import numpy as np
import ml_dtypes


def mxq(x, axis, fmt="e4m3"):
    dtype, down = {"e4m3": (ml_dtypes.float8_e4m3fn, 7), "e5m2": (ml_dtypes.float8_e5m2, 14)}[fmt]
    v = np.moveaxis(np.asarray(x, np.float32).astype(ml_dtypes.bfloat16).astype(np.float64), axis, -1)
    blocks = v.reshape(v.shape[:-1] + (-1, 32))
    amax = np.abs(blocks).max(-1, keepdims=True)
    byte = np.maximum(np.where(amax > 0, np.frexp(amax)[1] - 1 + 127, 0) - down, 1)
    scale = np.exp2(byte - 127.0)
    codes = (blocks / scale).astype(np.float32).astype(dtype).astype(np.float64)
    return np.moveaxis((codes * scale).reshape(v.shape), -1, axis)


WIDE = False


def mx_kscale(k):
    if not WIDE:
        return np.ones(k)
    levels = np.array([10, -10, 5, -5, 0])
    if k % 512:
        return np.exp2(np.random.permutation(np.resize(levels, k // 32))).repeat(32)
    a = np.empty((k // 512, 16))
    for p in range(k // 512):
        a[p, :8] = np.random.permutation(np.resize(levels, 8))
        for g in range(8):
            far = levels[np.abs(levels - a[p, g]) >= 10]
            a[p, g + 8] = far[np.random.randint(len(far))]
    return np.exp2(a.ravel()).repeat(32)


def f64(x):
    return np.asarray(x).astype(np.float64)


def striped(idx):
    return np.tile(idx.reshape(-1, 16).T, (8, 1)).astype(np.uint16)


def unstriped(offs):
    return offs[:16].T.reshape(-1).astype(np.int64)


K, T, E, C, N = 1536, 512, 8, 128, 256


def by_expert(wq, xq):
    return np.concatenate([wq[e].T @ xq[:, e * C:(e + 1) * C] for e in range(E)], axis=1)


def setup_inputs():
    n = np.random.standard_normal
    s = mx_kscale(K)[:, None]
    first = np.random.permutation(np.repeat(np.arange(E), T // E))
    second = (first + 1 + np.random.permutation(np.repeat(np.arange(E - 1), -(-T // (E - 1)))[:T])) % E
    while np.bincount(second, minlength=E).max() != T // E:
        load = np.bincount(second, minlength=E); hi, lo = int(load.argmax()), int(load.argmin())
        t = np.flatnonzero((second == hi) & (first != lo))[0]; second[t] = lo
    slot_token = np.empty(E * C, np.int64); pos = np.empty((2, T), np.int64); fill = np.zeros(E, np.int64)
    place = np.stack([np.random.permutation(C) for _ in range(E)])
    for r, deal in enumerate((first, second)):
        for t in np.random.permutation(T):
            e = deal[t]; j = e * C + place[e, fill[e]]; fill[e] += 1; slot_token[j] = t; pos[r, t] = j
    g = np.random.uniform(0.2, 0.8, T)
    return {
        "xT": (n((K, T)) * s).astype(np.float32),
        "w": (n((E, K, N)) / np.sqrt(K) / s[None]).astype(np.float32),
        "gate": np.stack([np.tile(g, (N, 1)), np.tile(1.0 - g, (N, 1))]).astype(np.float32),
        "offs": striped(slot_token),
        "pos1": striped(pos[0]),
        "pos2": striped(pos[1]),
    }


def reference(xT, w, gate, offs, pos1, pos2):
    idx = unstriped(offs)
    xq = mxq(f64(xT)[:, idx], 0, "e4m3")
    y = by_expert(mxq(f64(w), 1, "e4m3"), xq)
    return f64(gate[0]) * y[:, unstriped(pos1)] + f64(gate[1]) * y[:, unstriped(pos2)]

@@ -1,0 +1,189 @@
+from contextlib import ExitStack
+
+import concourse.mybir as mybir
+
+K, T, E, C, N = 1536, 512, 8, 128, 256
+SLOTS = E * C
+
+FLOPS = 2 * SLOTS * K * N
+BYTES = 4 * K * T + 4 * E * K * N + 4 * 2 * T + 2 * 128 * (SLOTS + 2 * T) // 16 + 4 * N * T
+
+F32 = mybir.dt.float32
+BF16 = mybir.dt.bfloat16
+U32 = mybir.dt.uint32
+U16 = mybir.dt.uint16
+U8 = mybir.dt.uint8
+FP8X4 = mybir.dt.float8_e4m3fn_x4
+MULT = mybir.AluOpType.mult
+ADD = mybir.AluOpType.add
+
+P = 128
+PACK = 4
+PASSES = K // (P * PACK)
+M = 128
+BLOCKS = N // M
+
+CHUNKS = [(0, 384), (384, 768), (768, 1024)]
+
+
+def interleave(copy, dst, src):
+    copy(
+        out=dst.rearrange("p (c i) j -> p c j i", i=4),
+        in_=src.rearrange("p j (c i) -> p c j i", i=4),
+    )
+
+
+def tile_routed_moe_kernel(tc, xT, w, gate, offs, pos1, pos2, out):
+    nc = tc.nc
+    vcopy = nc.vector.tensor_copy
+    scopy = nc.scalar.copy
+
+    x_view = xT.rearrange("(a p j) t -> a p j t", p=P, j=PACK)
+    w_view = w.rearrange("e (a p j) n -> e a p j n", p=P, j=PACK)
+
+    with ExitStack() as ctx:
+        lists = ctx.enter_context(tc.tile_pool(name="lists", bufs=1))
+        keep = ctx.enter_context(tc.tile_pool(name="keep", bufs=1))
+        wraw_pool = ctx.enter_context(tc.tile_pool(name="wraw", bufs=23))
+        w16_pool = ctx.enter_context(tc.tile_pool(name="w16", bufs=11))
+        psum = ctx.enter_context(tc.psum_pool(name="psum", bufs=1))
+
+        offs_sb = lists.tile([P, SLOTS // 16], U16, name="offs_sb")
+        pos1_sb = lists.tile([P, T // 16], U16, name="pos1_sb")
+        pos2_sb = lists.tile([P, T // 16], U16, name="pos2_sb")
+        gate_sb = keep.tile([P, 2, T], F32, name="gate_sb")
+
+        xraw = [keep.tile([P, PACK, T], F32, name=f"xraw{a}") for a in range(PASSES)]
+        x16 = [keep.tile([P, T, PACK], BF16, name=f"x16_{a}", align_bytes=64) for a in range(PASSES)]
+        xc = [keep.tile([P, T], U32, name=f"xc{a}", align_bytes=64) for a in range(PASSES)]
+        xs = [keep.tile([P, T], U8, name=f"xs{a}", align_bytes=64) for a in range(PASSES)]
+        gc = keep.tile([P, PASSES, SLOTS], U32, name="gc", align_bytes=64)
+        gs = keep.tile([P, PASSES, SLOTS], U8, name="gs", align_bytes=64)
+        wc = keep.tile([P, E * PASSES, N], U32, name="wc", align_bytes=64)
+        ws = keep.tile([P, E * PASSES, N], U8, name="ws", align_bytes=64)
+        y = [keep.tile([P, SLOTS], F32, name=f"y{b}") for b in range(BLOCKS)]
+
+        for a in range(PASSES):
+            nc.gpsimd.memset(xs[a][:], 0)
+
+        nc.sync.dma_start(xraw[0][:], x_view[0])
+        nc.sync.dma_start(offs_sb[:], offs)
+        nc.sync.dma_start(xraw[1][:], x_view[1])
+        nc.sync.dma_start(xraw[2][:], x_view[2])
+        wraw = {}
+        for e in range(E):
+            if e == E - 1:
+                nc.sync.dma_start(pos1_sb[:], pos1)
+                nc.sync.dma_start(pos2_sb[:], pos2)
+                nc.sync.dma_start(gate_sb[:], gate[:, 0:P, :].rearrange("g p t -> p g t"))
+            for a in range(PASSES):
+                if (e, a) == (E - 1, PASSES - 1):
+                    continue
+                raw = wraw_pool.tile([P, PACK, N], F32, name="raw")
+                nc.sync.dma_start(raw[:], w_view[e, a])
+                wraw[e, a] = raw
+        tail_raw = [keep.tile([P, PACK, M], F32, name=f"tail_raw{b}") for b in range(BLOCKS)]
+        for b in range(BLOCKS):
+            nc.sync.dma_start(tail_raw[b][:], w_view[E - 1, PASSES - 1, :, :, b * M : (b + 1) * M])
+
+        for a in range(PASSES):
+            h = T // 2
+            interleave(vcopy, x16[a][:, 0:h, :], xraw[a][:, :, 0:h])
+            interleave(scopy, x16[a][:, h:T, :], xraw[a][:, :, h:T])
+            nc.vector.quantize_mx(
+                out=xc[a][:].bitcast(FP8X4), scales=xs[a][:], in_=x16[a][:].rearrange("p t j -> p (t j)")
+            )
+
+        def gather(lo, hi):
+            cols = offs_sb[:, lo // 16 : hi // 16]
+            for a in range(PASSES):
+                nc.vector.tensor_copy(gc[:, a, lo:hi], xc[a][:].indirect(cols))
+                nc.vector.tensor_copy(gs[:, a, lo:hi], xs[a][:].indirect(cols))
+
+        def weights(e, a, copy):
+            w16 = w16_pool.tile([P, N, PACK], BF16, name="w16", align_bytes=64)
+            interleave(copy, w16[:], wraw[e, a][:])
+            u = e * PASSES + a
+            nc.vector.quantize_mx(
+                out=wc[:, u, :].bitcast(FP8X4), scales=ws[:, u, :], in_=w16[:].rearrange("p n j -> p (n j)")
+            )
+
+        groups = [(0, 4), (4, 7), (7, 8)]
+        banks = {}
+        for b in range(BLOCKS):
+            for q in range(len(groups)):
+                banks[b, q] = psum.tile([M, 512], F32, name=f"bank{b}{q}")
+
+        def bank_of(e):
+            return [q for q, g in enumerate(groups) if g[0] <= e < g[1]][0]
+
+        def multiply(e, b, passes=range(PASSES)):
+            q = bank_of(e)
+            col = (e - groups[q][0]) * C
+            for a in passes:
+                u = e * PASSES + a
+                nc.tensor.matmul_mx(
+                    out=banks[b, q][:, col : col + C],
+                    lhsT=wc[:, u, b * M : (b + 1) * M].bitcast(FP8X4),
+                    lhsT_scale=ws[:, u, b * M : (b + 1) * M],
+                    rhs=gc[:, a, e * C : (e + 1) * C].bitcast(FP8X4),
+                    rhs_scale=gs[:, a, e * C : (e + 1) * C],
+                    start=(a == 0),
+                    stop=(a == PASSES - 1),
+                )
+
+        def evacuate(copy, b, q):
+            lo, hi = groups[q]
+            copy(out=y[b][:, lo * C : hi * C], in_=banks[b, q][:, 0 : (hi - lo) * C])
+
+        gather_before = {0: 0, 2: 1, 5: 2}
+        for e in range(E - 1):
+            if e in gather_before:
+                gather(*CHUNKS[gather_before[e]])
+            for a in range(PASSES):
+                u = e * PASSES + a
+                weights(e, a, vcopy if u % 4 == 3 else scopy)
+            for b in range(BLOCKS):
+                multiply(e, b)
+            q = bank_of(e)
+            if e == groups[q][1] - 1:
+                for b in range(BLOCKS):
+                    evacuate(scopy, b, q)
+
+        e = E - 1
+        u = e * PASSES + PASSES - 1
+        weights(e, 0, scopy)
+        weights(e, 1, vcopy)
+
+        def tail_weights(b, copy):
+            w16t = keep.tile([P, M, PACK], BF16, name=f"w16t{b}", align_bytes=64)
+            interleave(copy, w16t[:], tail_raw[b][:])
+            cols = slice(b * M, (b + 1) * M)
+            nc.vector.quantize_mx(
+                out=wc[:, u, cols].bitcast(FP8X4), scales=ws[:, u, cols], in_=w16t[:].rearrange("p n j -> p (n j)")
+            )
+
+        first = [keep.tile([P, T], F32, name=f"first{b}") for b in range(BLOCKS)]
+        second = [keep.tile([P, T], F32, name=f"second{b}") for b in range(BLOCKS)]
+        total = [keep.tile([P, T], F32, name=f"total{b}") for b in range(BLOCKS)]
+
+        def fetch1(b):
+            nc.vector.tensor_tensor(first[b][:], y[b][:].indirect(pos1_sb[:]), gate_sb[:, 0, :], MULT)
+
+        def fetch2(b, lo, hi):
+            cols = pos2_sb[:, lo // 16 : hi // 16]
+            nc.vector.tensor_tensor(second[b][:, lo:hi], y[b][:].indirect(cols), gate_sb[:, 1, lo:hi], MULT)
+            nc.vector.tensor_tensor(total[b][:, lo:hi], first[b][:, lo:hi], second[b][:, lo:hi], ADD)
+            nc.sync.dma_start(out[b * M : (b + 1) * M, lo:hi], total[b][:, lo:hi])
+
+        tail_weights(0, vcopy)
+        multiply(e, 0)
+        evacuate(vcopy, 0, 2)
+        fetch1(0)
+        tail_weights(1, scopy)
+        multiply(e, 1)
+        evacuate(scopy, 1, 2)
+        fetch2(0, 0, T)
+        fetch1(1)
+        fetch2(1, 0, T // 2)
+        fetch2(1, T // 2, T)

@@ -23,6 +23,8 @@ PASSES = K // (P * PACK)
 M = 128
 BLOCKS = N // M
 
+ON_VECTOR = (8, 14, 19, 22)
+UNITS = [(u, u + 1) for u in range(0, 20, 2)] + [(20,), (21,), (22,)]
 CHUNKS = [(0, 384), (384, 768), (768, 1024)]
 
 
@@ -45,7 +47,7 @@ def tile_routed_moe_kernel(tc, xT, w, gate, offs, pos1, pos2, out):
         lists = ctx.enter_context(tc.tile_pool(name="lists", bufs=1))
         keep = ctx.enter_context(tc.tile_pool(name="keep", bufs=1))
         wraw_pool = ctx.enter_context(tc.tile_pool(name="wraw", bufs=23))
-        w16_pool = ctx.enter_context(tc.tile_pool(name="w16", bufs=11))
+        w16_pool = ctx.enter_context(tc.tile_pool(name="w16", bufs=6))
         psum = ctx.enter_context(tc.psum_pool(name="psum", bufs=1))
 
         offs_sb = lists.tile([P, SLOTS // 16], U16, name="offs_sb")
@@ -56,15 +58,14 @@ def tile_routed_moe_kernel(tc, xT, w, gate, offs, pos1, pos2, out):
         xraw = [keep.tile([P, PACK, T], F32, name=f"xraw{a}") for a in range(PASSES)]
         x16 = [keep.tile([P, T, PACK], BF16, name=f"x16_{a}", align_bytes=64) for a in range(PASSES)]
         xc = [keep.tile([P, T], U32, name=f"xc{a}", align_bytes=64) for a in range(PASSES)]
-        xs = [keep.tile([P, T], U8, name=f"xs{a}", align_bytes=64) for a in range(PASSES)]
+        xs = keep.tile([P, T], U8, name="xs", align_bytes=64)
         gc = keep.tile([P, PASSES, SLOTS], U32, name="gc", align_bytes=64)
-        gs = keep.tile([P, PASSES, SLOTS], U8, name="gs", align_bytes=64)
+        gs = keep.tile([P, SLOTS], U8, name="gs", align_bytes=64)
         wc = keep.tile([P, E * PASSES, N], U32, name="wc", align_bytes=64)
         ws = keep.tile([P, E * PASSES, N], U8, name="ws", align_bytes=64)
         y = [keep.tile([P, SLOTS], F32, name=f"y{b}") for b in range(BLOCKS)]
 
-        for a in range(PASSES):
-            nc.gpsimd.memset(xs[a][:], 0)
+        nc.gpsimd.memset(xs[:], 0)
 
         nc.sync.dma_start(xraw[0][:], x_view[0])
         nc.sync.dma_start(offs_sb[:], offs)
@@ -91,21 +92,24 @@ def tile_routed_moe_kernel(tc, xT, w, gate, offs, pos1, pos2, out):
             interleave(vcopy, x16[a][:, 0:h, :], xraw[a][:, :, 0:h])
             interleave(scopy, x16[a][:, h:T, :], xraw[a][:, :, h:T])
             nc.vector.quantize_mx(
-                out=xc[a][:].bitcast(FP8X4), scales=xs[a][:], in_=x16[a][:].rearrange("p t j -> p (t j)")
+                out=xc[a][:].bitcast(FP8X4), scales=xs[4 * a : P, :], in_=x16[a][:].rearrange("p t j -> p (t j)")
             )
 
         def gather(lo, hi):
             cols = offs_sb[:, lo // 16 : hi // 16]
             for a in range(PASSES):
                 nc.vector.tensor_copy(gc[:, a, lo:hi], xc[a][:].indirect(cols))
-                nc.vector.tensor_copy(gs[:, a, lo:hi], xs[a][:].indirect(cols))
+            nc.vector.tensor_copy(gs[:, lo:hi], xs[:].indirect(cols))
 
-        def weights(e, a, copy):
-            w16 = w16_pool.tile([P, N, PACK], BF16, name="w16", align_bytes=64)
-            interleave(copy, w16[:], wraw[e, a][:])
-            u = e * PASSES + a
+        def weights(units):
+            w16 = w16_pool.tile([P, 2, N, PACK], BF16, name="w16", align_bytes=64)
+            for i, u in enumerate(units):
+                interleave(vcopy if u in ON_VECTOR else scopy, w16[:, i], wraw[divmod(u, PASSES)][:])
+            lo, n = units[0], len(units)
             nc.vector.quantize_mx(
-                out=wc[:, u, :].bitcast(FP8X4), scales=ws[:, u, :], in_=w16[:].rearrange("p n j -> p (n j)")
+                out=wc[:, lo : lo + n, :].rearrange("p u n -> p (u n)").bitcast(FP8X4),
+                scales=ws[:, lo : lo + n, :].rearrange("p u n -> p (u n)"),
+                in_=w16[:, 0:n].rearrange("p u n j -> p (u n j)"),
             )
 
         groups = [(0, 4), (4, 7), (7, 8)]
@@ -127,7 +131,7 @@ def tile_routed_moe_kernel(tc, xT, w, gate, offs, pos1, pos2, out):
                     lhsT=wc[:, u, b * M : (b + 1) * M].bitcast(FP8X4),
                     lhsT_scale=ws[:, u, b * M : (b + 1) * M],
                     rhs=gc[:, a, e * C : (e + 1) * C].bitcast(FP8X4),
-                    rhs_scale=gs[:, a, e * C : (e + 1) * C],
+                    rhs_scale=gs[4 * a : P, e * C : (e + 1) * C],
                     start=(a == 0),
                     stop=(a == PASSES - 1),
                 )
@@ -136,24 +140,23 @@ def tile_routed_moe_kernel(tc, xT, w, gate, offs, pos1, pos2, out):
             lo, hi = groups[q]
             copy(out=y[b][:, lo * C : hi * C], in_=banks[b, q][:, 0 : (hi - lo) * C])
 
-        gather_before = {0: 0, 2: 1, 5: 2}
-        for e in range(E - 1):
-            if e in gather_before:
-                gather(*CHUNKS[gather_before[e]])
-            for a in range(PASSES):
-                u = e * PASSES + a
-                weights(e, a, vcopy if u % 4 == 3 else scopy)
-            for b in range(BLOCKS):
-                multiply(e, b)
-            q = bank_of(e)
-            if e == groups[q][1] - 1:
-                for b in range(BLOCKS):
-                    evacuate(scopy, b, q)
+        gather_before = {0: 0, 6: 1, 14: 2}
+        for units in UNITS:
+            if units[0] in gather_before:
+                gather(*CHUNKS[gather_before[units[0]]])
+            weights(units)
+            for u in units:
+                e, a = divmod(u, PASSES)
+                if a == PASSES - 1:
+                    for b in range(BLOCKS):
+                        multiply(e, b)
+                    q = bank_of(e)
+                    if e == groups[q][1] - 1:
+                        for b in range(BLOCKS):
+                            evacuate(scopy, b, q)
 
         e = E - 1
         u = e * PASSES + PASSES - 1
-        weights(e, 0, scopy)
-        weights(e, 1, vcopy)
 
         def tail_weights(b, copy):
             w16t = keep.tile([P, M, PACK], BF16, name=f"w16t{b}", align_bytes=64)

@@ -22,10 +22,25 @@ PACK = 4
 PASSES = K // (P * PACK)
 M = 128
 BLOCKS = N // M
+LAST = E - 1
+UNITS = LAST * PASSES
 
-ON_VECTOR = (8, 14, 19, 22)
-UNITS = [(u, u + 1) for u in range(0, 20, 2)] + [(20,), (21,), (22,)]
 CHUNKS = [(0, 384), (384, 768), (768, 1024)]
+SCALES = PASSES
+GATHER_X = {1: [(0, 0)], 2: [(0, 1)]}
+GATHER_W = {
+    1: [(0, 2), (0, SCALES)],
+    3: [(1, 0)],
+    5: [(1, 1), (1, 2)],
+    7: [(1, SCALES)],
+    9: [(2, 0), (2, 1)],
+    11: [(2, 2)],
+    13: [(2, SCALES)],
+}
+EVACUATE = {13: (0, 0), 15: (1, 0)}
+ON_VECTOR = (4, 8, 12, 16, 18, 20)
+X_SPLIT = 336
+GROUPS = [(0, 4), (4, 6), (6, 8)]
 
 
 def interleave(copy, dst, src):
@@ -41,13 +56,13 @@ def tile_routed_moe_kernel(tc, xT, w, gate, offs, pos1, pos2, out):
     scopy = nc.scalar.copy
 
     x_view = xT.rearrange("(a p j) t -> a p j t", p=P, j=PACK)
-    w_view = w.rearrange("e (a p j) n -> e a p j n", p=P, j=PACK)
+    w_view = w.rearrange("e (a p j) n -> (e a) p j n", p=P, j=PACK)
 
     with ExitStack() as ctx:
         lists = ctx.enter_context(tc.tile_pool(name="lists", bufs=1))
         keep = ctx.enter_context(tc.tile_pool(name="keep", bufs=1))
-        wraw_pool = ctx.enter_context(tc.tile_pool(name="wraw", bufs=23))
-        w16_pool = ctx.enter_context(tc.tile_pool(name="w16", bufs=6))
+        raw_pool = ctx.enter_context(tc.tile_pool(name="raw_pool", bufs=7))
+        grouped_pool = ctx.enter_context(tc.tile_pool(name="grouped_pool", bufs=8))
         psum = ctx.enter_context(tc.psum_pool(name="psum", bufs=1))
 
         offs_sb = lists.tile([P, SLOTS // 16], U16, name="offs_sb")
@@ -55,81 +70,100 @@ def tile_routed_moe_kernel(tc, xT, w, gate, offs, pos1, pos2, out):
         pos2_sb = lists.tile([P, T // 16], U16, name="pos2_sb")
         gate_sb = keep.tile([P, 2, T], F32, name="gate_sb")
 
-        xraw = [keep.tile([P, PACK, T], F32, name=f"xraw{a}") for a in range(PASSES)]
-        x16 = [keep.tile([P, T, PACK], BF16, name=f"x16_{a}", align_bytes=64) for a in range(PASSES)]
         xc = [keep.tile([P, T], U32, name=f"xc{a}", align_bytes=64) for a in range(PASSES)]
         xs = keep.tile([P, T], U8, name="xs", align_bytes=64)
         gc = keep.tile([P, PASSES, SLOTS], U32, name="gc", align_bytes=64)
         gs = keep.tile([P, SLOTS], U8, name="gs", align_bytes=64)
-        wc = keep.tile([P, E * PASSES, N], U32, name="wc", align_bytes=64)
-        ws = keep.tile([P, E * PASSES, N], U8, name="ws", align_bytes=64)
+        wc = keep.tile([P, UNITS, N], U32, name="wc", align_bytes=64)
+        ws = keep.tile([P, UNITS, N], U8, name="ws", align_bytes=64)
+        last_c = [keep.tile([P, PASSES, M], U32, name=f"last_c{b}", align_bytes=64) for b in range(BLOCKS)]
+        last_s = [keep.tile([P, PASSES, M], U8, name=f"last_s{b}", align_bytes=64) for b in range(BLOCKS)]
         y = [keep.tile([P, SLOTS], F32, name=f"y{b}") for b in range(BLOCKS)]
 
+        select = keep.tile([P, P], F32, name="select")
+        gate_rows = keep.tile([P, 2, T], F32, name="gate_rows")
+        nc.vector.memset(gate_rows[:], 0.0)
+        nc.gpsimd.memset(select[:], 0.0)
+        nc.gpsimd.memset(select[0:1, :], 1.0)
         nc.gpsimd.memset(xs[:], 0)
 
-        nc.sync.dma_start(xraw[0][:], x_view[0])
-        nc.sync.dma_start(offs_sb[:], offs)
-        nc.sync.dma_start(xraw[1][:], x_view[1])
-        nc.sync.dma_start(xraw[2][:], x_view[2])
         wraw = {}
-        for e in range(E):
-            if e == E - 1:
-                nc.sync.dma_start(pos1_sb[:], pos1)
-                nc.sync.dma_start(pos2_sb[:], pos2)
-                nc.sync.dma_start(gate_sb[:], gate[:, 0:P, :].rearrange("g p t -> p g t"))
-            for a in range(PASSES):
-                if (e, a) == (E - 1, PASSES - 1):
-                    continue
-                raw = wraw_pool.tile([P, PACK, N], F32, name="raw")
-                nc.sync.dma_start(raw[:], w_view[e, a])
-                wraw[e, a] = raw
-        tail_raw = [keep.tile([P, PACK, M], F32, name=f"tail_raw{b}") for b in range(BLOCKS)]
+
+        def load_x(a):
+            raw = raw_pool.tile([P, PACK, T], F32, name="raw")
+            nc.sync.dma_start(raw[:], x_view[a])
+            return raw
+
+        first_raw = raw_pool.tile([P, 1, PACK, N], F32, name="raw")
+        nc.sync.dma_start(first_raw[:, 0], w_view[0])
+        wraw[0] = first_raw[:, 0]
+        xraw = [load_x(0)]
+        nc.sync.dma_start(gate_rows[0:1, :, :], gate[:, 0:1, :].rearrange("g p t -> p g t"))
+        nc.sync.dma_start(offs_sb[:], offs)
+        xraw.append(load_x(1))
+        xraw.append(load_x(2))
+        for u in range(1, UNITS, 2):
+            raw = raw_pool.tile([P, 2, PACK, N], F32, name="raw")
+            nc.sync.dma_start(raw[:], w_view[u : u + 2].rearrange("u p j n -> p u j n"))
+            wraw[u] = raw[:, 0]
+            wraw[u + 1] = raw[:, 1]
+        nc.sync.dma_start(pos1_sb[:], pos1)
+        nc.sync.dma_start(pos2_sb[:], pos2)
+        last_raw = {}
         for b in range(BLOCKS):
-            nc.sync.dma_start(tail_raw[b][:], w_view[E - 1, PASSES - 1, :, :, b * M : (b + 1) * M])
+            cols = slice(b * M, (b + 1) * M)
+            for a in range(PASSES):
+                raw = keep.tile([P, PACK, M], F32, name=f"last_raw{b}{a}")
+                nc.sync.dma_start(raw[:], w_view[UNITS + a, :, :, cols])
+                last_raw[b, a] = raw
+
+        def quantise(codes, scales, grouped):
+            nc.vector.quantize_mx(out=codes.bitcast(FP8X4), scales=scales, in_=grouped)
+
+        grouped = grouped_pool.tile([P, N, PACK], BF16, name="grouped", align_bytes=64)
+        interleave(vcopy, grouped[:, 0:128, :], wraw[0][:, :, 0:128])
+        interleave(scopy, grouped[:, 128:N, :], wraw[0][:, :, 128:N])
+        quantise(wc[:, 0, :], ws[:, 0, :], grouped[:].rearrange("p n j -> p (n j)"))
+
+        def gather(chunk, part):
+            lo, hi = CHUNKS[chunk]
+            cols = offs_sb[:, lo // 16 : hi // 16]
+            if part == SCALES:
+                nc.vector.tensor_copy(gs[:, lo:hi], xs[:].indirect(cols))
+            else:
+                nc.vector.tensor_copy(gc[:, part, lo:hi], xc[part][:].indirect(cols))
 
         for a in range(PASSES):
-            h = T // 2
-            interleave(vcopy, x16[a][:, 0:h, :], xraw[a][:, :, 0:h])
-            interleave(scopy, x16[a][:, h:T, :], xraw[a][:, :, h:T])
-            nc.vector.quantize_mx(
-                out=xc[a][:].bitcast(FP8X4), scales=xs[4 * a : P, :], in_=x16[a][:].rearrange("p t j -> p (t j)")
-            )
+            grouped = grouped_pool.tile([P, T, PACK], BF16, name="grouped", align_bytes=64)
+            interleave(vcopy, grouped[:, 0:X_SPLIT, :], xraw[a][:, :, 0:X_SPLIT])
+            interleave(scopy, grouped[:, X_SPLIT:T, :], xraw[a][:, :, X_SPLIT:T])
+            for g in GATHER_X.get(a, []):
+                gather(*g)
+            quantise(xc[a][:], xs[4 * a : P, :], grouped[:].rearrange("p t j -> p (t j)"))
 
-        def gather(lo, hi):
-            cols = offs_sb[:, lo // 16 : hi // 16]
-            for a in range(PASSES):
-                nc.vector.tensor_copy(gc[:, a, lo:hi], xc[a][:].indirect(cols))
-            nc.vector.tensor_copy(gs[:, lo:hi], xs[:].indirect(cols))
+        for r in range(2):
+            gate_bank = psum.tile([P, T], F32, name=f"gate_bank{r}")
+            nc.tensor.matmul(gate_bank[:], select[:], gate_rows[:, r, :], start=True, stop=True)
+            scopy(out=gate_sb[:, r, :], in_=gate_bank[:])
 
-        def weights(units):
-            w16 = w16_pool.tile([P, 2, N, PACK], BF16, name="w16", align_bytes=64)
-            for i, u in enumerate(units):
-                interleave(vcopy if u in ON_VECTOR else scopy, w16[:, i], wraw[divmod(u, PASSES)][:])
-            lo, n = units[0], len(units)
-            nc.vector.quantize_mx(
-                out=wc[:, lo : lo + n, :].rearrange("p u n -> p (u n)").bitcast(FP8X4),
-                scales=ws[:, lo : lo + n, :].rearrange("p u n -> p (u n)"),
-                in_=w16[:, 0:n].rearrange("p u n j -> p (u n j)"),
-            )
-
-        groups = [(0, 4), (4, 7), (7, 8)]
         banks = {}
         for b in range(BLOCKS):
-            for q in range(len(groups)):
+            for q in range(len(GROUPS)):
                 banks[b, q] = psum.tile([M, 512], F32, name=f"bank{b}{q}")
 
         def bank_of(e):
-            return [q for q, g in enumerate(groups) if g[0] <= e < g[1]][0]
+            return [q for q, g in enumerate(GROUPS) if g[0] <= e < g[1]][0]
 
-        def multiply(e, b, passes=range(PASSES)):
+        def multiply(e, b):
             q = bank_of(e)
-            col = (e - groups[q][0]) * C
-            for a in passes:
+            col = (e - GROUPS[q][0]) * C
+            cols = slice(b * M, (b + 1) * M)
+            for a in range(PASSES):
                 u = e * PASSES + a
                 nc.tensor.matmul_mx(
                     out=banks[b, q][:, col : col + C],
-                    lhsT=wc[:, u, b * M : (b + 1) * M].bitcast(FP8X4),
-                    lhsT_scale=ws[:, u, b * M : (b + 1) * M],
+                    lhsT=(wc[:, u, cols] if e < LAST else last_c[b][:, a, :]).bitcast(FP8X4),
+                    lhsT_scale=ws[:, u, cols] if e < LAST else last_s[b][:, a, :],
                     rhs=gc[:, a, e * C : (e + 1) * C].bitcast(FP8X4),
                     rhs_scale=gs[4 * a : P, e * C : (e + 1) * C],
                     start=(a == 0),
@@ -137,33 +171,40 @@ def tile_routed_moe_kernel(tc, xT, w, gate, offs, pos1, pos2, out):
                 )
 
         def evacuate(copy, b, q):
-            lo, hi = groups[q]
+            lo, hi = GROUPS[q]
             copy(out=y[b][:, lo * C : hi * C], in_=banks[b, q][:, 0 : (hi - lo) * C])
 
-        gather_before = {0: 0, 6: 1, 14: 2}
-        for units in UNITS:
-            if units[0] in gather_before:
-                gather(*CHUNKS[gather_before[units[0]]])
-            weights(units)
-            for u in units:
+        for u0 in range(1, UNITS, 2):
+            grouped = grouped_pool.tile([P, 2, N, PACK], BF16, name="grouped", align_bytes=64)
+            for i in range(2):
+                interleave(vcopy if u0 + i in ON_VECTOR else scopy, grouped[:, i], wraw[u0 + i])
+            for g in GATHER_W.get(u0, []):
+                gather(*g)
+            quantise(
+                wc[:, u0 : u0 + 2, :].rearrange("p u n -> p (u n)"),
+                ws[:, u0 : u0 + 2, :].rearrange("p u n -> p (u n)"),
+                grouped[:].rearrange("p u n j -> p (u n j)"),
+            )
+            for u in (u0, u0 + 1):
                 e, a = divmod(u, PASSES)
                 if a == PASSES - 1:
                     for b in range(BLOCKS):
                         multiply(e, b)
-                    q = bank_of(e)
-                    if e == groups[q][1] - 1:
-                        for b in range(BLOCKS):
-                            evacuate(scopy, b, q)
+            if u0 in EVACUATE:
+                evacuate(scopy, *EVACUATE[u0])
 
-        e = E - 1
-        u = e * PASSES + PASSES - 1
+        last_grouped = [
+            keep.tile([P, PASSES, M, PACK], BF16, name=f"last_grouped{b}", align_bytes=64) for b in range(BLOCKS)
+        ]
 
-        def tail_weights(b, copy):
-            w16t = keep.tile([P, M, PACK], BF16, name=f"w16t{b}", align_bytes=64)
-            interleave(copy, w16t[:], tail_raw[b][:])
-            cols = slice(b * M, (b + 1) * M)
-            nc.vector.quantize_mx(
-                out=wc[:, u, cols].bitcast(FP8X4), scales=ws[:, u, cols], in_=w16t[:].rearrange("p n j -> p (n j)")
+        def last_interleave(b, a, copy):
+            interleave(copy, last_grouped[b][:, a], last_raw[b, a][:])
+
+        def last_quantise(b, lo, hi):
+            quantise(
+                last_c[b][:, lo:hi, :].rearrange("p a n -> p (a n)"),
+                last_s[b][:, lo:hi, :].rearrange("p a n -> p (a n)"),
+                last_grouped[b][:, lo:hi].rearrange("p a n j -> p (a n j)"),
             )
 
         first = [keep.tile([P, T], F32, name=f"first{b}") for b in range(BLOCKS)]
@@ -176,17 +217,33 @@ def tile_routed_moe_kernel(tc, xT, w, gate, offs, pos1, pos2, out):
         def fetch2(b, lo, hi):
             cols = pos2_sb[:, lo // 16 : hi // 16]
             nc.vector.tensor_tensor(second[b][:, lo:hi], y[b][:].indirect(cols), gate_sb[:, 1, lo:hi], MULT)
+
+        def finish(b, lo, hi):
             nc.vector.tensor_tensor(total[b][:, lo:hi], first[b][:, lo:hi], second[b][:, lo:hi], ADD)
             nc.sync.dma_start(out[b * M : (b + 1) * M, lo:hi], total[b][:, lo:hi])
 
-        tail_weights(0, vcopy)
-        multiply(e, 0)
+        last_interleave(0, 0, scopy)
+        last_interleave(0, 1, vcopy)
+        last_interleave(0, 2, vcopy)
+        evacuate(scopy, 0, 1)
+        last_quantise(0, 0, 2)
+        last_quantise(0, 2, 3)
+        multiply(LAST, 0)
+        last_interleave(1, 0, scopy)
+        last_interleave(1, 1, scopy)
         evacuate(vcopy, 0, 2)
         fetch1(0)
-        tail_weights(1, scopy)
-        multiply(e, 1)
+        last_quantise(1, 0, 2)
+        last_interleave(1, 2, scopy)
+        last_quantise(1, 2, 3)
+        multiply(LAST, 1)
+        evacuate(scopy, 1, 1)
         evacuate(scopy, 1, 2)
         fetch2(0, 0, T)
+        finish(0, 0, T)
         fetch1(1)
-        fetch2(1, 0, T // 2)
-        fetch2(1, T // 2, T)
+        h = T // 2
+        fetch2(1, 0, h)
+        finish(1, 0, h)
+        fetch2(1, h, T)
+        finish(1, h, T)

@@ -27,20 +27,18 @@ UNITS = LAST * PASSES
 
 CHUNKS = [(0, 384), (384, 768), (768, 1024)]
 SCALES = PASSES
-GATHER_X = {1: [(0, 0)], 2: [(0, 1)]}
-GATHER_W = {
-    1: [(0, 2), (0, SCALES)],
-    3: [(1, 0)],
-    5: [(1, 1), (1, 2)],
-    7: [(1, SCALES)],
-    9: [(2, 0), (2, 1)],
-    11: [(2, 2)],
-    13: [(2, SCALES)],
-}
-EVACUATE = {13: (0, 0), 15: (1, 0)}
-ON_VECTOR = (4, 8, 12, 16, 18, 20)
+GATHER_AFTER = {(1, 0): 1, (1, 1): 5, (1, 2): 7, (1, 3): 11, (2, 0): 9, (2, 1): 3, (2, 2): 11, (2, 3): 5}
+GATE_AFTER = 15
+RESULT_AFTER = (13, 19)
+ON_VECTOR = (4, 7, 12, 16, 17, 18, 19)
 X_SPLIT = 336
-GROUPS = [(0, 4), (4, 6), (6, 8)]
+LAST_HALVES = 3
+LAST_CUT = 384
+PE_ADD = 0
+LAST_ON_VECTOR = ((0, 2), (0, 1))
+RESULT_ON_VECTOR = ((0, 2),)
+LAST_QUANTISE = ((0, 1), (1, 2), (2, 3))
+GROUPS = [(0, 3), (3, 7), (7, 8)]
 
 
 def interleave(copy, dst, src):
@@ -61,24 +59,19 @@ def tile_routed_moe_kernel(tc, xT, w, gate, offs, pos1, pos2, out):
     with ExitStack() as ctx:
         lists = ctx.enter_context(tc.tile_pool(name="lists", bufs=1))
         keep = ctx.enter_context(tc.tile_pool(name="keep", bufs=1))
-        raw_pool = ctx.enter_context(tc.tile_pool(name="raw_pool", bufs=7))
-        grouped_pool = ctx.enter_context(tc.tile_pool(name="grouped_pool", bufs=8))
+        slots = ctx.enter_context(tc.tile_pool(name="slots", bufs=1))
         psum = ctx.enter_context(tc.psum_pool(name="psum", bufs=1))
 
         offs_sb = lists.tile([P, SLOTS // 16], U16, name="offs_sb")
         pos1_sb = lists.tile([P, T // 16], U16, name="pos1_sb")
         pos2_sb = lists.tile([P, T // 16], U16, name="pos2_sb")
-        gate_sb = keep.tile([P, 2, T], F32, name="gate_sb")
 
         xc = [keep.tile([P, T], U32, name=f"xc{a}", align_bytes=64) for a in range(PASSES)]
         xs = keep.tile([P, T], U8, name="xs", align_bytes=64)
-        gc = keep.tile([P, PASSES, SLOTS], U32, name="gc", align_bytes=64)
-        gs = keep.tile([P, SLOTS], U8, name="gs", align_bytes=64)
         wc = keep.tile([P, UNITS, N], U32, name="wc", align_bytes=64)
         ws = keep.tile([P, UNITS, N], U8, name="ws", align_bytes=64)
         last_c = [keep.tile([P, PASSES, M], U32, name=f"last_c{b}", align_bytes=64) for b in range(BLOCKS)]
         last_s = [keep.tile([P, PASSES, M], U8, name=f"last_s{b}", align_bytes=64) for b in range(BLOCKS)]
-        y = [keep.tile([P, SLOTS], F32, name=f"y{b}") for b in range(BLOCKS)]
 
         select = keep.tile([P, P], F32, name="select")
         gate_rows = keep.tile([P, 2, T], F32, name="gate_rows")
@@ -86,15 +79,16 @@ def tile_routed_moe_kernel(tc, xT, w, gate, offs, pos1, pos2, out):
         nc.gpsimd.memset(select[:], 0.0)
         nc.gpsimd.memset(select[0:1, :], 1.0)
         nc.gpsimd.memset(xs[:], 0)
+        identity = select
 
         wraw = {}
 
         def load_x(a):
-            raw = raw_pool.tile([P, PACK, T], F32, name="raw")
+            raw = slots.tile([P, PACK, T], F32, name=f"xraw{a}", align_bytes=64)
             nc.sync.dma_start(raw[:], x_view[a])
             return raw
 
-        first_raw = raw_pool.tile([P, 1, PACK, N], F32, name="raw")
+        first_raw = keep.tile([P, 1, PACK, N], F32, name="first_raw")
         nc.sync.dma_start(first_raw[:, 0], w_view[0])
         wraw[0] = first_raw[:, 0]
         xraw = [load_x(0)]
@@ -103,48 +97,62 @@ def tile_routed_moe_kernel(tc, xT, w, gate, offs, pos1, pos2, out):
         xraw.append(load_x(1))
         xraw.append(load_x(2))
         for u in range(1, UNITS, 2):
-            raw = raw_pool.tile([P, 2, PACK, N], F32, name="raw")
+            raw = slots.tile([P, 2, PACK, N], F32, name=f"raw{u}", align_bytes=64)
             nc.sync.dma_start(raw[:], w_view[u : u + 2].rearrange("u p j n -> p u j n"))
             wraw[u] = raw[:, 0]
             wraw[u + 1] = raw[:, 1]
         nc.sync.dma_start(pos1_sb[:], pos1)
         nc.sync.dma_start(pos2_sb[:], pos2)
         last_raw = {}
+        for a in range(PASSES - LAST_HALVES):
+            raw = keep.tile([P, PACK, N], F32, name=f"last_raw{a}")
+            nc.sync.dma_start(raw[:], w_view[UNITS + a])
+            for b in range(BLOCKS):
+                last_raw[b, a] = raw[:, :, b * M : (b + 1) * M]
         for b in range(BLOCKS):
             cols = slice(b * M, (b + 1) * M)
-            for a in range(PASSES):
+            for a in range(PASSES - LAST_HALVES, PASSES):
                 raw = keep.tile([P, PACK, M], F32, name=f"last_raw{b}{a}")
                 nc.sync.dma_start(raw[:], w_view[UNITS + a, :, :, cols])
-                last_raw[b, a] = raw
+                last_raw[b, a] = raw[:]
 
         def quantise(codes, scales, grouped):
             nc.vector.quantize_mx(out=codes.bitcast(FP8X4), scales=scales, in_=grouped)
 
-        grouped = grouped_pool.tile([P, N, PACK], BF16, name="grouped", align_bytes=64)
+        grouped = keep.tile([P, N, PACK], BF16, name="first_grouped", align_bytes=64)
         interleave(vcopy, grouped[:, 0:128, :], wraw[0][:, :, 0:128])
         interleave(scopy, grouped[:, 128:N, :], wraw[0][:, :, 128:N])
         quantise(wc[:, 0, :], ws[:, 0, :], grouped[:].rearrange("p n j -> p (n j)"))
 
+        gw = {}
+
         def gather(chunk, part):
             lo, hi = CHUNKS[chunk]
             cols = offs_sb[:, lo // 16 : hi // 16]
+            after = GATHER_AFTER.get((chunk, part))
             if part == SCALES:
-                nc.vector.tensor_copy(gs[:, lo:hi], xs[:].indirect(cols))
+                tag = f"raw{after}" if after else f"gs{chunk}"
+                tile = slots.tile([P, hi - lo], U8, name=f"gs{chunk}", tag=tag, align_bytes=64)
+                nc.vector.tensor_copy(tile[:], xs[:].indirect(cols))
             else:
-                nc.vector.tensor_copy(gc[:, part, lo:hi], xc[part][:].indirect(cols))
+                tag = f"grouped{after}" if after else f"gc{chunk}{part}"
+                tile = slots.tile([P, hi - lo], U32, name=f"gc{chunk}{part}", tag=tag, align_bytes=64)
+                nc.vector.tensor_copy(tile[:], xc[part][:].indirect(cols))
+            gw[chunk, part] = tile
 
         for a in range(PASSES):
-            grouped = grouped_pool.tile([P, T, PACK], BF16, name="grouped", align_bytes=64)
+            grouped = slots.tile([P, T, PACK], BF16, name=f"xgrouped{a}", align_bytes=64)
             interleave(vcopy, grouped[:, 0:X_SPLIT, :], xraw[a][:, :, 0:X_SPLIT])
             interleave(scopy, grouped[:, X_SPLIT:T, :], xraw[a][:, :, X_SPLIT:T])
-            for g in GATHER_X.get(a, []):
-                gather(*g)
             quantise(xc[a][:], xs[4 * a : P, :], grouped[:].rearrange("p t j -> p (t j)"))
+            gather(0, a)
+        gather(0, SCALES)
 
+        gate_banks = []
         for r in range(2):
             gate_bank = psum.tile([P, T], F32, name=f"gate_bank{r}")
             nc.tensor.matmul(gate_bank[:], select[:], gate_rows[:, r, :], start=True, stop=True)
-            scopy(out=gate_sb[:, r, :], in_=gate_bank[:])
+            gate_banks.append(gate_bank)
 
         banks = {}
         for b in range(BLOCKS):
@@ -157,6 +165,8 @@ def tile_routed_moe_kernel(tc, xT, w, gate, offs, pos1, pos2, out):
         def multiply(e, b):
             q = bank_of(e)
             col = (e - GROUPS[q][0]) * C
+            chunk = [i for i, c in enumerate(CHUNKS) if c[0] <= e * C < c[1]][0]
+            rows = slice(e * C - CHUNKS[chunk][0], (e + 1) * C - CHUNKS[chunk][0])
             cols = slice(b * M, (b + 1) * M)
             for a in range(PASSES):
                 u = e * PASSES + a
@@ -164,41 +174,51 @@ def tile_routed_moe_kernel(tc, xT, w, gate, offs, pos1, pos2, out):
                     out=banks[b, q][:, col : col + C],
                     lhsT=(wc[:, u, cols] if e < LAST else last_c[b][:, a, :]).bitcast(FP8X4),
                     lhsT_scale=ws[:, u, cols] if e < LAST else last_s[b][:, a, :],
-                    rhs=gc[:, a, e * C : (e + 1) * C].bitcast(FP8X4),
-                    rhs_scale=gs[4 * a : P, e * C : (e + 1) * C],
+                    rhs=gw[chunk, a][:, rows].bitcast(FP8X4),
+                    rhs_scale=gw[chunk, SCALES][4 * a : P, rows],
                     start=(a == 0),
                     stop=(a == PASSES - 1),
                 )
 
+        y = {}
+
         def evacuate(copy, b, q):
             lo, hi = GROUPS[q]
+            if q == 0:
+                y[b] = slots.tile([P, SLOTS], F32, name=f"y{b}", tag=f"raw{RESULT_AFTER[b]}", align_bytes=64)
             copy(out=y[b][:, lo * C : hi * C], in_=banks[b, q][:, 0 : (hi - lo) * C])
 
         for u0 in range(1, UNITS, 2):
-            grouped = grouped_pool.tile([P, 2, N, PACK], BF16, name="grouped", align_bytes=64)
+            grouped = slots.tile([P, 2, N, PACK], BF16, name=f"grouped{u0}", align_bytes=64)
             for i in range(2):
                 interleave(vcopy if u0 + i in ON_VECTOR else scopy, grouped[:, i], wraw[u0 + i])
-            for g in GATHER_W.get(u0, []):
-                gather(*g)
             quantise(
                 wc[:, u0 : u0 + 2, :].rearrange("p u n -> p (u n)"),
                 ws[:, u0 : u0 + 2, :].rearrange("p u n -> p (u n)"),
                 grouped[:].rearrange("p u n j -> p (u n j)"),
             )
+            for g, after in GATHER_AFTER.items():
+                if after == u0:
+                    gather(*g)
             for u in (u0, u0 + 1):
                 e, a = divmod(u, PASSES)
                 if a == PASSES - 1:
                     for b in range(BLOCKS):
                         multiply(e, b)
-            if u0 in EVACUATE:
-                evacuate(scopy, *EVACUATE[u0])
+            if u0 == GATE_AFTER:
+                gate_sb = slots.tile([P, 2, T], F32, name="gate_sb", tag=f"raw{u0}", align_bytes=64)
+                for r in range(2):
+                    scopy(out=gate_sb[:, r, :], in_=gate_banks[r][:])
+            for b in range(BLOCKS):
+                if u0 == max(RESULT_AFTER[b], 11):
+                    evacuate(scopy, b, 0)
 
         last_grouped = [
             keep.tile([P, PASSES, M, PACK], BF16, name=f"last_grouped{b}", align_bytes=64) for b in range(BLOCKS)
         ]
 
         def last_interleave(b, a, copy):
-            interleave(copy, last_grouped[b][:, a], last_raw[b, a][:])
+            interleave(copy, last_grouped[b][:, a], last_raw[b, a])
 
         def last_quantise(b, lo, hi):
             quantise(
@@ -207,9 +227,9 @@ def tile_routed_moe_kernel(tc, xT, w, gate, offs, pos1, pos2, out):
                 last_grouped[b][:, lo:hi].rearrange("p a n j -> p (a n j)"),
             )
 
-        first = [keep.tile([P, T], F32, name=f"first{b}") for b in range(BLOCKS)]
-        second = [keep.tile([P, T], F32, name=f"second{b}") for b in range(BLOCKS)]
-        total = [keep.tile([P, T], F32, name=f"total{b}") for b in range(BLOCKS)]
+        first = [slots.tile([P, T], F32, name=f"first{b}", tag=f"raw{1 + 2 * b}", align_bytes=64) for b in range(BLOCKS)]
+        second = [slots.tile([P, T], F32, name=f"second{b}", tag=("raw7", "xraw2")[b], align_bytes=64) for b in range(BLOCKS)]
+        total = [slots.tile([P, T], F32, name=f"total{b}", tag=f"xraw{b}", align_bytes=64) for b in range(BLOCKS)]
 
         def fetch1(b):
             nc.vector.tensor_tensor(first[b][:], y[b][:].indirect(pos1_sb[:]), gate_sb[:, 0, :], MULT)
@@ -218,31 +238,39 @@ def tile_routed_moe_kernel(tc, xT, w, gate, offs, pos1, pos2, out):
             cols = pos2_sb[:, lo // 16 : hi // 16]
             nc.vector.tensor_tensor(second[b][:, lo:hi], y[b][:].indirect(cols), gate_sb[:, 1, lo:hi], MULT)
 
+        def add_on_tensor(b):
+            bank = psum.tile([P, T], F32, name="gate_bank0")
+            nc.tensor.matmul(bank[:], identity[:], first[b][:], start=True, stop=False)
+            nc.tensor.matmul(bank[:], identity[:], second[b][:], start=False, stop=True)
+            scopy(out=total[b][:], in_=bank[:])
+            nc.sync.dma_start(out[b * M : (b + 1) * M, :], total[b][:])
+
         def finish(b, lo, hi):
             nc.vector.tensor_tensor(total[b][:, lo:hi], first[b][:, lo:hi], second[b][:, lo:hi], ADD)
             nc.sync.dma_start(out[b * M : (b + 1) * M, lo:hi], total[b][:, lo:hi])
 
-        last_interleave(0, 0, scopy)
-        last_interleave(0, 1, vcopy)
-        last_interleave(0, 2, vcopy)
-        evacuate(scopy, 0, 1)
-        last_quantise(0, 0, 2)
-        last_quantise(0, 2, 3)
+        for a in range(PASSES):
+            last_interleave(0, a, vcopy if (0, a) in LAST_ON_VECTOR else scopy)
+        evacuate(vcopy if (0, 1) in RESULT_ON_VECTOR else scopy, 0, 1)
+        for lo, hi in LAST_QUANTISE:
+            last_quantise(0, lo, hi)
         multiply(LAST, 0)
-        last_interleave(1, 0, scopy)
-        last_interleave(1, 1, scopy)
-        evacuate(vcopy, 0, 2)
+        evacuate(vcopy if (0, 2) in RESULT_ON_VECTOR else scopy, 0, 2)
+        for a in range(PASSES):
+            last_interleave(1, a, vcopy if (1, a) in LAST_ON_VECTOR else scopy)
         fetch1(0)
-        last_quantise(1, 0, 2)
-        last_interleave(1, 2, scopy)
-        last_quantise(1, 2, 3)
+        for lo, hi in LAST_QUANTISE:
+            last_quantise(1, lo, hi)
         multiply(LAST, 1)
-        evacuate(scopy, 1, 1)
-        evacuate(scopy, 1, 2)
+        evacuate(vcopy if (1, 1) in RESULT_ON_VECTOR else scopy, 1, 1)
+        evacuate(vcopy if (1, 2) in RESULT_ON_VECTOR else scopy, 1, 2)
         fetch2(0, 0, T)
-        finish(0, 0, T)
+        if PE_ADD:
+            add_on_tensor(0)
+        else:
+            finish(0, 0, T)
         fetch1(1)
-        h = T // 2
+        h = LAST_CUT
         fetch2(1, 0, h)
         finish(1, 0, h)
         fetch2(1, h, T)

from contextlib import ExitStack

import concourse.mybir as mybir

K, T, E, C, N = 1536, 512, 8, 128, 256
SLOTS = E * C

FLOPS = 2 * SLOTS * K * N
BYTES = 4 * K * T + 4 * E * K * N + 4 * 2 * T + 2 * 128 * (SLOTS + 2 * T) // 16 + 4 * N * T

F32 = mybir.dt.float32
BF16 = mybir.dt.bfloat16
U32 = mybir.dt.uint32
U16 = mybir.dt.uint16
U8 = mybir.dt.uint8
FP8X4 = mybir.dt.float8_e4m3fn_x4
MULT = mybir.AluOpType.mult
ADD = mybir.AluOpType.add

P = 128
PACK = 4
PASSES = K // (P * PACK)
M = 128
BLOCKS = N // M
LAST = E - 1
UNITS = LAST * PASSES

CHUNKS = [(0, 384), (384, 768), (768, 1024)]
SCALES = PASSES
GATHER_AFTER = {(1, 0): 1, (1, 1): 5, (1, 2): 7, (1, 3): 11, (2, 0): 9, (2, 1): 3, (2, 2): 11, (2, 3): 5}
GATE_AFTER = 15
RESULT_AFTER = (13, 19)
ON_VECTOR = (4, 7, 12, 16, 17, 18, 19)
X_SPLIT = 336
LAST_HALVES = 3
LAST_CUT = 384
PE_ADD = 0
LAST_ON_VECTOR = ((0, 2), (0, 1))
RESULT_ON_VECTOR = ((0, 2),)
LAST_QUANTISE = ((0, 1), (1, 2), (2, 3))
GROUPS = [(0, 3), (3, 7), (7, 8)]


def interleave(copy, dst, src):
    copy(
        out=dst.rearrange("p (c i) j -> p c j i", i=4),
        in_=src.rearrange("p j (c i) -> p c j i", i=4),
    )


def tile_routed_moe_kernel(tc, xT, w, gate, offs, pos1, pos2, out):
    nc = tc.nc
    vcopy = nc.vector.tensor_copy
    scopy = nc.scalar.copy

    x_view = xT.rearrange("(a p j) t -> a p j t", p=P, j=PACK)
    w_view = w.rearrange("e (a p j) n -> (e a) p j n", p=P, j=PACK)

    with ExitStack() as ctx:
        lists = ctx.enter_context(tc.tile_pool(name="lists", bufs=1))
        keep = ctx.enter_context(tc.tile_pool(name="keep", bufs=1))
        slots = ctx.enter_context(tc.tile_pool(name="slots", bufs=1))
        psum = ctx.enter_context(tc.psum_pool(name="psum", bufs=1))

        offs_sb = lists.tile([P, SLOTS // 16], U16, name="offs_sb")
        pos1_sb = lists.tile([P, T // 16], U16, name="pos1_sb")
        pos2_sb = lists.tile([P, T // 16], U16, name="pos2_sb")

        xc = [keep.tile([P, T], U32, name=f"xc{a}", align_bytes=64) for a in range(PASSES)]
        xs = keep.tile([P, T], U8, name="xs", align_bytes=64)
        wc = keep.tile([P, UNITS, N], U32, name="wc", align_bytes=64)
        ws = keep.tile([P, UNITS, N], U8, name="ws", align_bytes=64)
        last_c = [keep.tile([P, PASSES, M], U32, name=f"last_c{b}", align_bytes=64) for b in range(BLOCKS)]
        last_s = [keep.tile([P, PASSES, M], U8, name=f"last_s{b}", align_bytes=64) for b in range(BLOCKS)]

        select = keep.tile([P, P], F32, name="select")
        gate_rows = keep.tile([P, 2, T], F32, name="gate_rows")
        nc.vector.memset(gate_rows[:], 0.0)
        nc.gpsimd.memset(select[:], 0.0)
        nc.gpsimd.memset(select[0:1, :], 1.0)
        nc.gpsimd.memset(xs[:], 0)
        identity = select

        wraw = {}

        def load_x(a):
            raw = slots.tile([P, PACK, T], F32, name=f"xraw{a}", align_bytes=64)
            nc.sync.dma_start(raw[:], x_view[a])
            return raw

        first_raw = keep.tile([P, 1, PACK, N], F32, name="first_raw")
        nc.sync.dma_start(first_raw[:, 0], w_view[0])
        wraw[0] = first_raw[:, 0]
        xraw = [load_x(0)]
        nc.sync.dma_start(gate_rows[0:1, :, :], gate[:, 0:1, :].rearrange("g p t -> p g t"))
        nc.sync.dma_start(offs_sb[:], offs)
        xraw.append(load_x(1))
        xraw.append(load_x(2))
        for u in range(1, UNITS, 2):
            raw = slots.tile([P, 2, PACK, N], F32, name=f"raw{u}", align_bytes=64)
            nc.sync.dma_start(raw[:], w_view[u : u + 2].rearrange("u p j n -> p u j n"))
            wraw[u] = raw[:, 0]
            wraw[u + 1] = raw[:, 1]
        nc.sync.dma_start(pos1_sb[:], pos1)
        nc.sync.dma_start(pos2_sb[:], pos2)
        last_raw = {}
        for a in range(PASSES - LAST_HALVES):
            raw = keep.tile([P, PACK, N], F32, name=f"last_raw{a}")
            nc.sync.dma_start(raw[:], w_view[UNITS + a])
            for b in range(BLOCKS):
                last_raw[b, a] = raw[:, :, b * M : (b + 1) * M]
        for b in range(BLOCKS):
            cols = slice(b * M, (b + 1) * M)
            for a in range(PASSES - LAST_HALVES, PASSES):
                raw = keep.tile([P, PACK, M], F32, name=f"last_raw{b}{a}")
                nc.sync.dma_start(raw[:], w_view[UNITS + a, :, :, cols])
                last_raw[b, a] = raw[:]

        def quantise(codes, scales, grouped):
            nc.vector.quantize_mx(out=codes.bitcast(FP8X4), scales=scales, in_=grouped)

        grouped = keep.tile([P, N, PACK], BF16, name="first_grouped", align_bytes=64)
        interleave(vcopy, grouped[:, 0:128, :], wraw[0][:, :, 0:128])
        interleave(scopy, grouped[:, 128:N, :], wraw[0][:, :, 128:N])
        quantise(wc[:, 0, :], ws[:, 0, :], grouped[:].rearrange("p n j -> p (n j)"))

        gw = {}

        def gather(chunk, part):
            lo, hi = CHUNKS[chunk]
            cols = offs_sb[:, lo // 16 : hi // 16]
            after = GATHER_AFTER.get((chunk, part))
            if part == SCALES:
                tag = f"raw{after}" if after else f"gs{chunk}"
                tile = slots.tile([P, hi - lo], U8, name=f"gs{chunk}", tag=tag, align_bytes=64)
                nc.vector.tensor_copy(tile[:], xs[:].indirect(cols))
            else:
                tag = f"grouped{after}" if after else f"gc{chunk}{part}"
                tile = slots.tile([P, hi - lo], U32, name=f"gc{chunk}{part}", tag=tag, align_bytes=64)
                nc.vector.tensor_copy(tile[:], xc[part][:].indirect(cols))
            gw[chunk, part] = tile

        for a in range(PASSES):
            grouped = slots.tile([P, T, PACK], BF16, name=f"xgrouped{a}", align_bytes=64)
            interleave(vcopy, grouped[:, 0:X_SPLIT, :], xraw[a][:, :, 0:X_SPLIT])
            interleave(scopy, grouped[:, X_SPLIT:T, :], xraw[a][:, :, X_SPLIT:T])
            quantise(xc[a][:], xs[4 * a : P, :], grouped[:].rearrange("p t j -> p (t j)"))
            gather(0, a)
        gather(0, SCALES)

        gate_banks = []
        for r in range(2):
            gate_bank = psum.tile([P, T], F32, name=f"gate_bank{r}")
            nc.tensor.matmul(gate_bank[:], select[:], gate_rows[:, r, :], start=True, stop=True)
            gate_banks.append(gate_bank)

        banks = {}
        for b in range(BLOCKS):
            for q in range(len(GROUPS)):
                banks[b, q] = psum.tile([M, 512], F32, name=f"bank{b}{q}")

        def bank_of(e):
            return [q for q, g in enumerate(GROUPS) if g[0] <= e < g[1]][0]

        def multiply(e, b):
            q = bank_of(e)
            col = (e - GROUPS[q][0]) * C
            chunk = [i for i, c in enumerate(CHUNKS) if c[0] <= e * C < c[1]][0]
            rows = slice(e * C - CHUNKS[chunk][0], (e + 1) * C - CHUNKS[chunk][0])
            cols = slice(b * M, (b + 1) * M)
            for a in range(PASSES):
                u = e * PASSES + a
                nc.tensor.matmul_mx(
                    out=banks[b, q][:, col : col + C],
                    lhsT=(wc[:, u, cols] if e < LAST else last_c[b][:, a, :]).bitcast(FP8X4),
                    lhsT_scale=ws[:, u, cols] if e < LAST else last_s[b][:, a, :],
                    rhs=gw[chunk, a][:, rows].bitcast(FP8X4),
                    rhs_scale=gw[chunk, SCALES][4 * a : P, rows],
                    start=(a == 0),
                    stop=(a == PASSES - 1),
                )

        y = {}

        def evacuate(copy, b, q):
            lo, hi = GROUPS[q]
            if q == 0:
                y[b] = slots.tile([P, SLOTS], F32, name=f"y{b}", tag=f"raw{RESULT_AFTER[b]}", align_bytes=64)
            copy(out=y[b][:, lo * C : hi * C], in_=banks[b, q][:, 0 : (hi - lo) * C])

        for u0 in range(1, UNITS, 2):
            grouped = slots.tile([P, 2, N, PACK], BF16, name=f"grouped{u0}", align_bytes=64)
            for i in range(2):
                interleave(vcopy if u0 + i in ON_VECTOR else scopy, grouped[:, i], wraw[u0 + i])
            quantise(
                wc[:, u0 : u0 + 2, :].rearrange("p u n -> p (u n)"),
                ws[:, u0 : u0 + 2, :].rearrange("p u n -> p (u n)"),
                grouped[:].rearrange("p u n j -> p (u n j)"),
            )
            for g, after in GATHER_AFTER.items():
                if after == u0:
                    gather(*g)
            for u in (u0, u0 + 1):
                e, a = divmod(u, PASSES)
                if a == PASSES - 1:
                    for b in range(BLOCKS):
                        multiply(e, b)
            if u0 == GATE_AFTER:
                gate_sb = slots.tile([P, 2, T], F32, name="gate_sb", tag=f"raw{u0}", align_bytes=64)
                for r in range(2):
                    scopy(out=gate_sb[:, r, :], in_=gate_banks[r][:])
            for b in range(BLOCKS):
                if u0 == max(RESULT_AFTER[b], 11):
                    evacuate(scopy, b, 0)

        last_grouped = [
            keep.tile([P, PASSES, M, PACK], BF16, name=f"last_grouped{b}", align_bytes=64) for b in range(BLOCKS)
        ]

        def last_interleave(b, a, copy):
            interleave(copy, last_grouped[b][:, a], last_raw[b, a])

        def last_quantise(b, lo, hi):
            quantise(
                last_c[b][:, lo:hi, :].rearrange("p a n -> p (a n)"),
                last_s[b][:, lo:hi, :].rearrange("p a n -> p (a n)"),
                last_grouped[b][:, lo:hi].rearrange("p a n j -> p (a n j)"),
            )

        first = [slots.tile([P, T], F32, name=f"first{b}", tag=f"raw{1 + 2 * b}", align_bytes=64) for b in range(BLOCKS)]
        second = [slots.tile([P, T], F32, name=f"second{b}", tag=("raw7", "xraw2")[b], align_bytes=64) for b in range(BLOCKS)]
        total = [slots.tile([P, T], F32, name=f"total{b}", tag=f"xraw{b}", align_bytes=64) for b in range(BLOCKS)]

        def fetch1(b):
            nc.vector.tensor_tensor(first[b][:], y[b][:].indirect(pos1_sb[:]), gate_sb[:, 0, :], MULT)

        def fetch2(b, lo, hi):
            cols = pos2_sb[:, lo // 16 : hi // 16]
            nc.vector.tensor_tensor(second[b][:, lo:hi], y[b][:].indirect(cols), gate_sb[:, 1, lo:hi], MULT)

        def add_on_tensor(b):
            bank = psum.tile([P, T], F32, name="gate_bank0")
            nc.tensor.matmul(bank[:], identity[:], first[b][:], start=True, stop=False)
            nc.tensor.matmul(bank[:], identity[:], second[b][:], start=False, stop=True)
            scopy(out=total[b][:], in_=bank[:])
            nc.sync.dma_start(out[b * M : (b + 1) * M, :], total[b][:])

        def finish(b, lo, hi):
            nc.vector.tensor_tensor(total[b][:, lo:hi], first[b][:, lo:hi], second[b][:, lo:hi], ADD)
            nc.sync.dma_start(out[b * M : (b + 1) * M, lo:hi], total[b][:, lo:hi])

        for a in range(PASSES):
            last_interleave(0, a, vcopy if (0, a) in LAST_ON_VECTOR else scopy)
        evacuate(vcopy if (0, 1) in RESULT_ON_VECTOR else scopy, 0, 1)
        for lo, hi in LAST_QUANTISE:
            last_quantise(0, lo, hi)
        multiply(LAST, 0)
        evacuate(vcopy if (0, 2) in RESULT_ON_VECTOR else scopy, 0, 2)
        for a in range(PASSES):
            last_interleave(1, a, vcopy if (1, a) in LAST_ON_VECTOR else scopy)
        fetch1(0)
        for lo, hi in LAST_QUANTISE:
            last_quantise(1, lo, hi)
        multiply(LAST, 1)
        evacuate(vcopy if (1, 1) in RESULT_ON_VECTOR else scopy, 1, 1)
        evacuate(vcopy if (1, 2) in RESULT_ON_VECTOR else scopy, 1, 2)
        fetch2(0, 0, T)
        if PE_ADD:
            add_on_tensor(0)
        else:
            finish(0, 0, T)
        fetch1(1)
        h = LAST_CUT
        fetch2(1, 0, h)
        finish(1, 0, h)
        fetch2(1, h, T)
        finish(1, h, T)
